import numpy as np
CORES = [97,101,225,229,353,357,481,485]
N = 8
W, TIMES = 64, 2
def setup_inputs(rng):
    return {"b": rng.standard_normal((N, 128, W), dtype=np.float32)}
def op(p):
    return 3.0 * p - (np.roll(p, 1, 1) + np.roll(p, -1, 1)) - 0.25 * (np.roll(p, 2, 1) + np.roll(p, -2, 1))
def reference(b):
    e = np.concatenate(list(b.astype(np.float64)), axis=1)
    x = np.zeros_like(e); p = e.copy(); ee = (e * e).sum(axis=1, keepdims=True)
    for _ in range(TIMES):
        q = op(p)
        al = ee / (p * q).sum(axis=1, keepdims=True)
        x = x + al * p; e = e - al * q
        en = (e * e).sum(axis=1, keepdims=True)
        p = e + (en / ee) * p; ee = en
    return {"y": np.stack([x[:, W * i:W * i + W] for i in range(N)]).astype(np.float32)}

@@ -1,0 +1,204 @@
+from concourse.bass import DstId, RemoteDMATransfer
+from concourse.mybir import AluOpType, AxisListType, ActivationFunctionType
+
+PW = 18
+SW = 2 * PW
+NSEM = 64
+SCRATCH = {
+    "G": ("sbuf", [128, 9, SW], "float32"),
+    "BP": ("sbuf", [128, 72], "float32"),
+    "DD": ("sbuf", [128, 3, 72], "float32"),
+    "SS": ("sbuf", [128, 3, 72], "float32"),
+    "J0": ("sbuf", [128, 4, 72], "float32"),
+    "PE": ("sbuf", [128, 5, PW], "float32"),
+    "JE": ("sbuf", [128, 5, PW], "float32"),
+    "PR": ("sbuf", [128, 4, PW], "float32"),
+    "JR": ("sbuf", [128, 4, PW], "float32"),
+    "WB": ("sbuf", [128, 2, 4], "float32"),
+    "PQ": ("sbuf", [128, 12], "float32"),
+    "TM": ("sbuf", [128, 4], "float32"),
+    "R3": ("sbuf", [128, 4], "float32"),
+    "D4W": ("sbuf", [128, 64], "float32"),
+    "T2": ("sbuf", [128, 64], "float32"),
+    "SB": ("sbuf", [128, 64], "float32"),
+    "YB": ("sbuf", [128, 64], "float32"),
+    "PT0": ("psum", [128, 512], "float32"),
+    "PT1": ("psum", [128, 512], "float32"),
+    "PT2": ("psum", [128, 512], "float32"),
+    "PT3": ("psum", [128, 512], "float32"),
+}
+SEMAPHORES = ["ld", "st", "sent", "arrL", "arrR", "arrP", "arrD"] + ["s%d" % i for i in range(NSEM)]
+
+W1, W2, W3 = -1.0 / 18.0, 1.0 / 324.0, -1.0 / 5832.0
+
+
+def _bits(mask):
+    return [e for e in range(16) if (mask >> e) & 1]
+
+
+def _mask(engines):
+    m = 0
+    for e in engines:
+        m |= 1 << e
+    return m
+
+
+def rank_program(g, core, T, topo):
+    rank = T.rank_of(core)
+    if rank is None:
+        return
+    n = len(T.cores)
+    V, A, S = g.vector, g.scalar, g.sync
+    add, sub, mul = AluOpType.add, AluOpType.subtract, AluOpType.mult
+    Ident, Square = ActivationFunctionType.Identity, ActivationFunctionType.Square
+    G, BP, DD, SS, J0, PE, JE, PR, JR, WB, PQ, TM = T.G, T.BP, T.DD, T.SS, T.J0, T.PE, T.JE, T.PR, T.JR, T.WB, T.PQ, T.TM
+    PT = [T.PT0, T.PT1, T.PT2]
+
+    mine = [r for r in range(n) if topo.host(T.cores[r]) == topo.host(core)]
+    base, first = mine[0], rank == mine[0]
+    per = len(mine)
+    partner = [r for r in mine if r != rank][0]
+    nxt = [(base + per + i) % n for i in range(per)]
+    prv = [(base - per + i) % n for i in range(per)]
+    p = per + (rank - base)
+
+    cnt = [0]
+
+    def done(instr):
+        s = T.sem["s%d" % cnt[0]]
+        cnt[0] += 1
+        instr.then_inc(s, 1)
+        return s
+
+    def wait(q, *sems):
+        for s in sems:
+            q.wait_ge(s, 1)
+
+    S.dma_start(BP[:, 4:68], T.b[:, :]).then_inc(T.sem.ld, 16)
+    z1 = done(V.memset(BP[:, 0:4], 0.0))
+    z2 = done(V.memset(BP[:, 68:72], 0.0))
+    zd = done(V.memset(DD[:, 0:2, :], 0.0))
+    k1 = done(V.memset(G[:, p, 0:2], 1.0))
+    k2 = done(V.memset(G[:, p, 10:11], 1.0))
+    k3 = done(V.memset(G[:, p, 11:12], W3))
+    zp = done(V.memset(PR[:, 3, :], 0.0))
+    wait(V, z1, z2, zd)
+    wait(A, z1, z2, zd)
+    V.wait_ge(T.sem.ld, 16)
+    A.wait_ge(T.sem.ld, 16)
+
+    sq = []
+    dk = None
+    for k in (1, 2, 3):
+        lo, hi = 4 - k, 68 + k
+        if k == 1:
+            left, right, mid = BP[:, lo - 1:hi - 1], BP[:, lo + 1:hi + 1], BP[:, lo:hi]
+        else:
+            left, right, mid = DD[:, k - 2, lo - 1:hi - 1], DD[:, k - 2, lo + 1:hi + 1], DD[:, k - 2, lo:hi]
+            wait(V, dk)
+            wait(A, dk)
+        sk = done(V.tensor_tensor(SS[:, k - 1, lo:hi], left, right, add))
+        tk = done(A.activation(PT[k - 1][:, lo:hi], mid, Ident, scale=2.0))
+        if k == 1:
+            sq.append(done(A.activation(J0[:, 0, 4:68], BP[:, 4:68], Square, accum_out=G[:, p, PW:PW + 1])))
+        elif k == 2:
+            sq.append(done(A.activation(J0[:, 1, 3:69], DD[:, 0, 3:69], Square, accum_out=G[:, p, PW + 1:PW + 2])))
+        else:
+            sq.append(done(A.activation(J0[:, 2, 2:70], DD[:, 1, 2:70], Square, accum_out=G[:, p, PW + 10:PW + 11])))
+            sq.append(done(A.activation(G[:, p, 2:10], DD[:, 0:2, 2:6], Ident, scale=2.0)))
+        wait(V, sk, tk)
+        dk = done(V.tensor_tensor(DD[:, k - 1, lo:hi], SS[:, k - 1, lo:hi], PT[k - 1][:, lo:hi], add))
+    wait(V, dk)
+    wait(A, dk)
+    c1 = done(V.tensor_copy(G[:, p, PW + 12:PW + 18], DD[:, 2, 65:71]))
+    c2 = done(V.tensor_scalar(G[:, p, 12:18], DD[:, 2, 1:7], 2.0 * W3, None, mul))
+    sq.append(done(A.activation(J0[:, 3, 1:71], DD[:, 2, 1:71], Square, accum_out=G[:, p, PW + 11:PW + 12])))
+    sq.append(done(A.activation(G[:, p, PW + 2:PW + 10], DD[:, 0:2, 66:70], Ident)))
+    own = [k1, k2, k3, c1, c2] + sq
+
+    def tr(dst_rank, engines, sem, slot):
+        d = T.cores[dst_rank]
+        rid, pid = topo.addr(d, core)
+        return RemoteDMATransfer(dst_ids=[DstId(rid=rid, pnc=pid)], dma_engine_mask=_mask(engines), remote_sem=sem,
+                                 src=G[:, p, :], dst=G[:, slot, :])
+
+    off = _bits(topo.mask(core, T.cores[nxt[0]]) & topo.mask(core, T.cores[prv[0]]))
+    onl = [e for e in _bits(topo.mask(core, T.cores[partner])) if e not in off]
+    half = len(off) // 2
+    ea, eb = off[:half], off[half:]
+    ep = onl[:half]
+    at_next = rank - base
+    at_prev = 2 * per + (rank - base)
+    wait(g, *own)
+    g.remote_dma_fused([tr(nxt[0], ea, T.sem.arrL, at_next), tr(prv[-1], eb, T.sem.arrR, at_prev)], local_sem=T.sem.sent)
+    g.remote_dma_fused([tr(nxt[-1], ea, T.sem.arrL, at_next), tr(prv[0], eb, T.sem.arrR, at_prev),
+                        tr(partner, ep, T.sem.arrP, p)], local_sem=T.sem.sent)
+    if first:
+        g.wait_ge(T.sem.arrL, per * half)
+        src, d = G[:, 0:per, :], T.cores[nxt[0]]
+    else:
+        g.wait_ge(T.sem.arrR, per * half)
+        src, d = G[:, 2 * per:3 * per, :], T.cores[prv[-1]]
+    rid, pid = topo.addr(d, core)
+    g.remote_dma(G[:, 3 * per:4 * per, :], src, T.sem.arrD, T.sem.sent, pid, rid, _mask(off))
+    g.wait_ge(T.sem.sent, 2 * half + 3 * half + len(off))
+
+    d4 = done(A.activation(T.D4W[:, :], DD[:, 1, 4:68], Ident, scale=W1))
+    A.wait_ge(T.sem.arrL, per * half)
+    c8 = done(A.activation(G[:, 8, 0:PW], G[:, 0, 0:PW], Ident))
+    V.wait_ge(T.sem.arrL, per * half)
+    V.wait_ge(T.sem.arrR, per * half)
+    V.wait_ge(T.sem.arrP, half)
+    wait(V, *own)
+    pe = done(V.tensor_tensor(PE[:, :, :], G[:, 0:5, PW:SW], G[:, 1:6, 0:PW], mul))
+    tl = done(V.tensor_scalar(TM[:, 0:2], G[:, p - 1, PW + 8:PW + 10], W1, None, mul))
+    t_r = done(V.tensor_scalar(TM[:, 2:4], G[:, p + 1, 6:8], 0.5 * W1, None, mul))
+    wait(V, d4, tl, t_r)
+    hl = done(V.tensor_tensor(T.D4W[:, 0:2], T.D4W[:, 0:2], TM[:, 0:2], add))
+    hr = done(V.tensor_tensor(T.D4W[:, 62:64], T.D4W[:, 62:64], TM[:, 2:4], add))
+    A.wait_ge(T.sem.arrR, per * half)
+    A.wait_ge(T.sem.arrP, half)
+    wait(A, pe, zp, *own)
+    e0 = done(A.activation(JE[:, :, 0], G[:, 0:5, PW], Ident, accum_out=G[:, 8, PW:PW + 1]))
+    e1 = done(A.activation(JE[:, :, 1:6], PE[:, :, 1:6], Ident, accum_out=PR[:, 3, 1:2]))
+    e2 = done(A.activation(JE[:, :, 6:11], PE[:, :, 6:11], Ident, accum_out=PR[:, 3, 6:7]))
+    e3 = done(A.activation(JE[:, :, 11:18], PE[:, :, 11:18], Ident, accum_out=T.R3[:, 3:4]))
+
+    V.wait_ge(T.sem.arrD, len(off))
+    wait(V, c8)
+    pl = done(V.tensor_tensor(PR[:, 0:3, :], G[:, 5:8, PW:SW], G[:, 6:9, 0:PW], mul))
+    A.wait_ge(T.sem.arrD, len(off))
+    wait(A, e0)
+    r0 = done(A.activation(JR[:, :, 0], G[:, 5:9, PW], Ident, accum_out=WB[:, 0, 0:1]))
+    wait(V, pl)
+    ra = done(V.tensor_reduce(T.R3[:, 0:3], PR[:, 0:3, 11:18], AxisListType.X, add))
+    wait(V, ra, e3)
+    r3 = done(V.tensor_reduce(WB[:, 0, 3:4], T.R3[:, 0:4], AxisListType.X, add))
+    wait(A, pl, e1, e2)
+    r1 = done(A.activation(JR[:, :, 1:6], PR[:, :, 1:6], Ident, scale=W1, accum_out=WB[:, 0, 1:2]))
+    r2 = done(A.activation(JR[:, :, 6:11], PR[:, :, 6:11], Ident, scale=W2, accum_out=WB[:, 0, 2:3]))
+    wait(V, r0, r1, r2, r3)
+    o2 = done(V.tensor_tensor(WB[:, 1, 0:3], WB[:, 0, 0:3], WB[:, 0, 1:4], add))
+    wait(V, o2)
+    wait(A, o2, r0, r1)
+    pp = done(V.tensor_scalar(PQ[:, 0:2], WB[:, :, 0], WB[:, 1, 2:3], None, mul))
+    qq = done(A.activation(PQ[:, 2:4], WB[:, :, 1], Ident, scale=WB[:, 1, 1:2]))
+    wait(V, pp, qq)
+    nd = done(V.tensor_tensor(PQ[:, 4:6], PQ[:, 0:2], PQ[:, 2:4], sub))
+    wait(V, nd)
+    rc = done(V.reciprocal(PQ[:, 6:7], PQ[:, 5:6]))
+    n1 = done(A.activation(PQ[:, 8:9], WB[:, 1, 1:2], Ident, scale=-1.0))
+    wait(A, n1)
+    n2 = done(A.activation(PQ[:, 9:10], WB[:, 0, 0:1], Ident, scale=PQ[:, 8:9]))
+    wait(A, n2)
+    n3 = done(A.activation(PQ[:, 10:11], WB[:, 0, 1:2], Ident, bias=PQ[:, 9:10], scale=WB[:, 1, 0:1]))
+    wait(A, n3, hl, hr, nd)
+    t1 = done(A.activation(T.PT3[:, 0:64], BP[:, 4:68], Ident, scale=PQ[:, 4:5]))
+    t2 = done(A.activation(T.T2[:, :], T.D4W[:, :], Ident, scale=PQ[:, 10:11]))
+    wait(V, t1, t2)
+    sm = done(V.tensor_tensor(T.SB[:, :], T.T2[:, :], T.PT3[:, 0:64], add))
+    wait(V, sm, rc)
+    yy = done(V.tensor_scalar(T.YB[:, :], T.SB[:, :], PQ[:, 6:7], 1.0 / 4.5, mul, mul))
+    wait(S, yy)
+    S.dma_start(T.y[:, :], T.YB[:, :]).then_inc(T.sem.st, 16)
+    S.wait_ge(T.sem.st, 16)

@@ -1,9 +1,9 @@
 from concourse.bass import DstId, RemoteDMATransfer
-from concourse.mybir import AluOpType, AxisListType, ActivationFunctionType
+from concourse.mybir import AluOpType, ActivationFunctionType
 
 PW = 18
 SW = 2 * PW
-NSEM = 64
+NSEM = 56
 SCRATCH = {
     "G": ("sbuf", [128, 9, SW], "float32"),
     "BP": ("sbuf", [128, 72], "float32"),
@@ -14,10 +14,10 @@ SCRATCH = {
     "JE": ("sbuf", [128, 5, PW], "float32"),
     "PR": ("sbuf", [128, 4, PW], "float32"),
     "JR": ("sbuf", [128, 4, PW], "float32"),
-    "WB": ("sbuf", [128, 2, 4], "float32"),
-    "PQ": ("sbuf", [128, 12], "float32"),
+    "NN": ("sbuf", [128, 4], "float32"),
+    "UV": ("sbuf", [128, 2, 4], "float32"),
+    "HH": ("sbuf", [128, 4], "float32"),
     "TM": ("sbuf", [128, 4], "float32"),
-    "R3": ("sbuf", [128, 4], "float32"),
     "D4W": ("sbuf", [128, 64], "float32"),
     "T2": ("sbuf", [128, 64], "float32"),
     "SB": ("sbuf", [128, 64], "float32"),
@@ -27,7 +27,7 @@ SCRATCH = {
     "PT2": ("psum", [128, 512], "float32"),
     "PT3": ("psum", [128, 512], "float32"),
 }
-SEMAPHORES = ["ld", "st", "sent", "arrL", "arrR", "arrP", "arrD"] + ["s%d" % i for i in range(NSEM)]
+SEMAPHORES = ["ld", "st", "sent", "arrL", "arrR", "arrP", "arrD", "pkg"] + ["s%d" % i for i in range(NSEM)]
 
 W1, W2, W3 = -1.0 / 18.0, 1.0 / 324.0, -1.0 / 5832.0
 
@@ -51,7 +51,8 @@ def rank_program(g, core, T, topo):
     V, A, S = g.vector, g.scalar, g.sync
     add, sub, mul = AluOpType.add, AluOpType.subtract, AluOpType.mult
     Ident, Square = ActivationFunctionType.Identity, ActivationFunctionType.Square
-    G, BP, DD, SS, J0, PE, JE, PR, JR, WB, PQ, TM = T.G, T.BP, T.DD, T.SS, T.J0, T.PE, T.JE, T.PR, T.JR, T.WB, T.PQ, T.TM
+    G, BP, DD, SS, J0, PE, JE, PR, JR, NN, UV, HH, TM = (T.G, T.BP, T.DD, T.SS, T.J0, T.PE, T.JE, T.PR, T.JR, T.NN, T.UV,
+                                                         T.HH, T.TM)
     PT = [T.PT0, T.PT1, T.PT2]
 
     mine = [r for r in range(n) if topo.host(T.cores[r]) == topo.host(core)]
@@ -63,12 +64,17 @@ def rank_program(g, core, T, topo):
     p = per + (rank - base)
 
     cnt = [0]
+    npk = [0]
 
     def done(instr):
         s = T.sem["s%d" % cnt[0]]
         cnt[0] += 1
         instr.then_inc(s, 1)
         return s
+
+    def part(instr):
+        npk[0] += 1
+        instr.then_inc(T.sem.pkg, 1)
 
     def wait(q, *sems):
         for s in sems:
@@ -78,16 +84,14 @@ def rank_program(g, core, T, topo):
     z1 = done(V.memset(BP[:, 0:4], 0.0))
     z2 = done(V.memset(BP[:, 68:72], 0.0))
     zd = done(V.memset(DD[:, 0:2, :], 0.0))
-    k1 = done(V.memset(G[:, p, 0:2], 1.0))
-    k2 = done(V.memset(G[:, p, 10:11], 1.0))
-    k3 = done(V.memset(G[:, p, 11:12], W3))
+    part(V.memset(G[:, p, 0:2], 0.5))
+    part(V.memset(G[:, p, 10:12], 0.5))
     zp = done(V.memset(PR[:, 3, :], 0.0))
     wait(V, z1, z2, zd)
     wait(A, z1, z2, zd)
     V.wait_ge(T.sem.ld, 16)
     A.wait_ge(T.sem.ld, 16)
 
-    sq = []
     dk = None
     for k in (1, 2, 3):
         lo, hi = 4 - k, 68 + k
@@ -100,21 +104,20 @@ def rank_program(g, core, T, topo):
         sk = done(V.tensor_tensor(SS[:, k - 1, lo:hi], left, right, add))
         tk = done(A.activation(PT[k - 1][:, lo:hi], mid, Ident, scale=2.0))
         if k == 1:
-            sq.append(done(A.activation(J0[:, 0, 4:68], BP[:, 4:68], Square, accum_out=G[:, p, PW:PW + 1])))
+            part(A.activation(J0[:, 0, 4:68], BP[:, 4:68], Square, accum_out=G[:, p, PW:PW + 1]))
         elif k == 2:
-            sq.append(done(A.activation(J0[:, 1, 3:69], DD[:, 0, 3:69], Square, accum_out=G[:, p, PW + 1:PW + 2])))
+            part(A.activation(J0[:, 1, 3:69], DD[:, 0, 3:69], Square, accum_out=G[:, p, PW + 1:PW + 2]))
         else:
-            sq.append(done(A.activation(J0[:, 2, 2:70], DD[:, 1, 2:70], Square, accum_out=G[:, p, PW + 10:PW + 11])))
-            sq.append(done(A.activation(G[:, p, 2:10], DD[:, 0:2, 2:6], Ident, scale=2.0)))
-        wait(V, sk, tk)
+            part(A.activation(J0[:, 2, 2:70], DD[:, 1, 2:70], Square, accum_out=G[:, p, PW + 10:PW + 11]))
+            part(A.activation(G[:, p, 2:10], DD[:, 0:2, 2:6], Ident))
+            part(A.activation(G[:, p, PW + 2:PW + 10], DD[:, 0:2, 66:70], Ident))
+        wait(V, tk, sk)
         dk = done(V.tensor_tensor(DD[:, k - 1, lo:hi], SS[:, k - 1, lo:hi], PT[k - 1][:, lo:hi], add))
-    wait(V, dk)
+    part(V.tensor_tensor(G[:, p, PW + 12:PW + 18], SS[:, 2, 65:71], T.PT2[:, 65:71], add))
+    part(V.tensor_tensor(G[:, p, 12:18], SS[:, 2, 1:7], T.PT2[:, 1:7], add))
     wait(A, dk)
-    c1 = done(V.tensor_copy(G[:, p, PW + 12:PW + 18], DD[:, 2, 65:71]))
-    c2 = done(V.tensor_scalar(G[:, p, 12:18], DD[:, 2, 1:7], 2.0 * W3, None, mul))
-    sq.append(done(A.activation(J0[:, 3, 1:71], DD[:, 2, 1:71], Square, accum_out=G[:, p, PW + 11:PW + 12])))
-    sq.append(done(A.activation(G[:, p, PW + 2:PW + 10], DD[:, 0:2, 66:70], Ident)))
-    own = [k1, k2, k3, c1, c2] + sq
+    part(A.activation(J0[:, 3, 1:71], DD[:, 2, 1:71], Square, accum_out=G[:, p, PW + 11:PW + 12]))
+    whole = npk[0]
 
     def tr(dst_rank, engines, sem, slot):
         d = T.cores[dst_rank]
@@ -129,7 +132,7 @@ def rank_program(g, core, T, topo):
     ep = onl[:half]
     at_next = rank - base
     at_prev = 2 * per + (rank - base)
-    wait(g, *own)
+    g.wait_ge(T.sem.pkg, whole)
     g.remote_dma_fused([tr(nxt[0], ea, T.sem.arrL, at_next), tr(prv[-1], eb, T.sem.arrR, at_prev)], local_sem=T.sem.sent)
     g.remote_dma_fused([tr(nxt[-1], ea, T.sem.arrL, at_next), tr(prv[0], eb, T.sem.arrR, at_prev),
                         tr(partner, ep, T.sem.arrP, p)], local_sem=T.sem.sent)
@@ -143,62 +146,55 @@ def rank_program(g, core, T, topo):
     g.remote_dma(G[:, 3 * per:4 * per, :], src, T.sem.arrD, T.sem.sent, pid, rid, _mask(off))
     g.wait_ge(T.sem.sent, 2 * half + 3 * half + len(off))
 
-    d4 = done(A.activation(T.D4W[:, :], DD[:, 1, 4:68], Ident, scale=W1))
+    d4 = done(A.activation(T.D4W[:, :], DD[:, 1, 4:68], Ident, scale=-W1))
     A.wait_ge(T.sem.arrL, per * half)
     c8 = done(A.activation(G[:, 8, 0:PW], G[:, 0, 0:PW], Ident))
+    V.wait_ge(T.sem.pkg, whole)
     V.wait_ge(T.sem.arrL, per * half)
     V.wait_ge(T.sem.arrR, per * half)
     V.wait_ge(T.sem.arrP, half)
-    wait(V, *own)
     pe = done(V.tensor_tensor(PE[:, :, :], G[:, 0:5, PW:SW], G[:, 1:6, 0:PW], mul))
-    tl = done(V.tensor_scalar(TM[:, 0:2], G[:, p - 1, PW + 8:PW + 10], W1, None, mul))
-    t_r = done(V.tensor_scalar(TM[:, 2:4], G[:, p + 1, 6:8], 0.5 * W1, None, mul))
+    tl = done(V.tensor_scalar(TM[:, 0:2], G[:, p - 1, PW + 8:PW + 10], -W1, None, mul))
+    t_r = done(V.tensor_scalar(TM[:, 2:4], G[:, p + 1, 6:8], -W1, None, mul))
     wait(V, d4, tl, t_r)
     hl = done(V.tensor_tensor(T.D4W[:, 0:2], T.D4W[:, 0:2], TM[:, 0:2], add))
     hr = done(V.tensor_tensor(T.D4W[:, 62:64], T.D4W[:, 62:64], TM[:, 2:4], add))
+    A.wait_ge(T.sem.pkg, whole)
     A.wait_ge(T.sem.arrR, per * half)
     A.wait_ge(T.sem.arrP, half)
-    wait(A, pe, zp, *own)
+    wait(A, zp, pe)
     e0 = done(A.activation(JE[:, :, 0], G[:, 0:5, PW], Ident, accum_out=G[:, 8, PW:PW + 1]))
     e1 = done(A.activation(JE[:, :, 1:6], PE[:, :, 1:6], Ident, accum_out=PR[:, 3, 1:2]))
     e2 = done(A.activation(JE[:, :, 6:11], PE[:, :, 6:11], Ident, accum_out=PR[:, 3, 6:7]))
-    e3 = done(A.activation(JE[:, :, 11:18], PE[:, :, 11:18], Ident, accum_out=T.R3[:, 3:4]))
+    e3 = done(A.activation(JE[:, :, 11:18], PE[:, :, 11:18], Ident, accum_out=PR[:, 3, 11:12]))
 
-    V.wait_ge(T.sem.arrD, len(off))
     wait(V, c8)
+    V.wait_ge(T.sem.arrD, len(off))
     pl = done(V.tensor_tensor(PR[:, 0:3, :], G[:, 5:8, PW:SW], G[:, 6:9, 0:PW], mul))
+    wait(A, e0, e1, e2, e3, hl, hr)
     A.wait_ge(T.sem.arrD, len(off))
-    wait(A, e0)
-    r0 = done(A.activation(JR[:, :, 0], G[:, 5:9, PW], Ident, accum_out=WB[:, 0, 0:1]))
-    wait(V, pl)
-    ra = done(V.tensor_reduce(T.R3[:, 0:3], PR[:, 0:3, 11:18], AxisListType.X, add))
-    wait(V, ra, e3)
-    r3 = done(V.tensor_reduce(WB[:, 0, 3:4], T.R3[:, 0:4], AxisListType.X, add))
-    wait(A, pl, e1, e2)
-    r1 = done(A.activation(JR[:, :, 1:6], PR[:, :, 1:6], Ident, scale=W1, accum_out=WB[:, 0, 1:2]))
-    r2 = done(A.activation(JR[:, :, 6:11], PR[:, :, 6:11], Ident, scale=W2, accum_out=WB[:, 0, 2:3]))
+    r0 = done(A.activation(JR[:, :, 0], G[:, 5:9, PW], Ident, scale=0.5, accum_out=NN[:, 0:1]))
+    wait(A, pl)
+    r1 = done(A.activation(JR[:, :, 1:6], PR[:, :, 1:6], Ident, scale=W1, accum_out=NN[:, 1:2]))
+    r2 = done(A.activation(JR[:, :, 6:11], PR[:, :, 6:11], Ident, scale=W2, accum_out=NN[:, 2:3]))
+    r3 = done(A.activation(JR[:, :, 11:18], PR[:, :, 11:18], Ident, scale=W3, accum_out=NN[:, 3:4]))
     wait(V, r0, r1, r2, r3)
-    o2 = done(V.tensor_tensor(WB[:, 1, 0:3], WB[:, 0, 0:3], WB[:, 0, 1:4], add))
-    wait(V, o2)
-    wait(A, o2, r0, r1)
-    pp = done(V.tensor_scalar(PQ[:, 0:2], WB[:, :, 0], WB[:, 1, 2:3], None, mul))
-    qq = done(A.activation(PQ[:, 2:4], WB[:, :, 1], Ident, scale=WB[:, 1, 1:2]))
-    wait(V, pp, qq)
-    nd = done(V.tensor_tensor(PQ[:, 4:6], PQ[:, 0:2], PQ[:, 2:4], sub))
-    wait(V, nd)
-    rc = done(V.reciprocal(PQ[:, 6:7], PQ[:, 5:6]))
-    n1 = done(A.activation(PQ[:, 8:9], WB[:, 1, 1:2], Ident, scale=-1.0))
-    wait(A, n1)
-    n2 = done(A.activation(PQ[:, 9:10], WB[:, 0, 0:1], Ident, scale=PQ[:, 8:9]))
-    wait(A, n2)
-    n3 = done(A.activation(PQ[:, 10:11], WB[:, 0, 1:2], Ident, bias=PQ[:, 9:10], scale=WB[:, 1, 0:1]))
-    wait(A, n3, hl, hr, nd)
-    t1 = done(A.activation(T.PT3[:, 0:64], BP[:, 4:68], Ident, scale=PQ[:, 4:5]))
-    t2 = done(A.activation(T.T2[:, :], T.D4W[:, :], Ident, scale=PQ[:, 10:11]))
+    wait(A, r1, r2)
+    u1 = done(V.tensor_scalar(UV[:, 0, 0:2], NN[:, 2:4], NN[:, 0:1], None, mul))
+    u2 = done(V.tensor_scalar(UV[:, 0, 2:3], NN[:, 3:4], NN[:, 1:2], None, mul))
+    v1 = done(A.activation(UV[:, 1, 0:2], NN[:, 1:3], Ident, scale=NN[:, 1:2]))
+    v2 = done(A.activation(UV[:, 1, 2:3], NN[:, 2:3], Ident, scale=NN[:, 2:3]))
+    wait(V, u1, u2, v1, v2)
+    hh = done(V.tensor_tensor_scan(HH[:, 0:3], UV[:, 0, 0:3], UV[:, 1, 0:3], 0.0, add, sub))
+    wait(V, hh)
+    wait(A, hh)
+    rc = done(V.reciprocal(HH[:, 3:4], HH[:, 2:3]))
+    t1 = done(A.activation(T.PT3[:, 0:64], BP[:, 4:68], Ident, scale=HH[:, 1:2]))
+    t2 = done(A.activation(T.T2[:, :], T.D4W[:, :], Ident, scale=HH[:, 0:1]))
     wait(V, t1, t2)
     sm = done(V.tensor_tensor(T.SB[:, :], T.T2[:, :], T.PT3[:, 0:64], add))
-    wait(V, sm, rc)
-    yy = done(V.tensor_scalar(T.YB[:, :], T.SB[:, :], PQ[:, 6:7], 1.0 / 4.5, mul, mul))
+    wait(V, rc, sm)
+    yy = done(V.tensor_scalar(T.YB[:, :], T.SB[:, :], HH[:, 3:4], 1.0 / 4.5, mul, mul))
     wait(S, yy)
     S.dma_start(T.y[:, :], T.YB[:, :]).then_inc(T.sem.st, 16)
     S.wait_ge(T.sem.st, 16)

from concourse.bass import DstId, RemoteDMATransfer
from concourse.mybir import AluOpType, ActivationFunctionType

PW = 18
SW = 2 * PW
NSEM = 56
SCRATCH = {
    "G": ("sbuf", [128, 9, SW], "float32"),
    "BP": ("sbuf", [128, 72], "float32"),
    "DD": ("sbuf", [128, 3, 72], "float32"),
    "SS": ("sbuf", [128, 3, 72], "float32"),
    "J0": ("sbuf", [128, 4, 72], "float32"),
    "PE": ("sbuf", [128, 5, PW], "float32"),
    "JE": ("sbuf", [128, 5, PW], "float32"),
    "PR": ("sbuf", [128, 4, PW], "float32"),
    "JR": ("sbuf", [128, 4, PW], "float32"),
    "NN": ("sbuf", [128, 4], "float32"),
    "UV": ("sbuf", [128, 2, 4], "float32"),
    "HH": ("sbuf", [128, 4], "float32"),
    "TM": ("sbuf", [128, 4], "float32"),
    "D4W": ("sbuf", [128, 64], "float32"),
    "T2": ("sbuf", [128, 64], "float32"),
    "SB": ("sbuf", [128, 64], "float32"),
    "YB": ("sbuf", [128, 64], "float32"),
    "PT0": ("psum", [128, 512], "float32"),
    "PT1": ("psum", [128, 512], "float32"),
    "PT2": ("psum", [128, 512], "float32"),
    "PT3": ("psum", [128, 512], "float32"),
}
SEMAPHORES = ["ld", "st", "sent", "arrL", "arrR", "arrP", "arrD", "pkg"] + ["s%d" % i for i in range(NSEM)]

W1, W2, W3 = -1.0 / 18.0, 1.0 / 324.0, -1.0 / 5832.0


def _bits(mask):
    return [e for e in range(16) if (mask >> e) & 1]


def _mask(engines):
    m = 0
    for e in engines:
        m |= 1 << e
    return m


def rank_program(g, core, T, topo):
    rank = T.rank_of(core)
    if rank is None:
        return
    n = len(T.cores)
    V, A, S = g.vector, g.scalar, g.sync
    add, sub, mul = AluOpType.add, AluOpType.subtract, AluOpType.mult
    Ident, Square = ActivationFunctionType.Identity, ActivationFunctionType.Square
    G, BP, DD, SS, J0, PE, JE, PR, JR, NN, UV, HH, TM = (T.G, T.BP, T.DD, T.SS, T.J0, T.PE, T.JE, T.PR, T.JR, T.NN, T.UV,
                                                         T.HH, T.TM)
    PT = [T.PT0, T.PT1, T.PT2]

    mine = [r for r in range(n) if topo.host(T.cores[r]) == topo.host(core)]
    base, first = mine[0], rank == mine[0]
    per = len(mine)
    partner = [r for r in mine if r != rank][0]
    nxt = [(base + per + i) % n for i in range(per)]
    prv = [(base - per + i) % n for i in range(per)]
    p = per + (rank - base)

    cnt = [0]
    npk = [0]

    def done(instr):
        s = T.sem["s%d" % cnt[0]]
        cnt[0] += 1
        instr.then_inc(s, 1)
        return s

    def part(instr):
        npk[0] += 1
        instr.then_inc(T.sem.pkg, 1)

    def wait(q, *sems):
        for s in sems:
            q.wait_ge(s, 1)

    S.dma_start(BP[:, 4:68], T.b[:, :]).then_inc(T.sem.ld, 16)
    z1 = done(V.memset(BP[:, 0:4], 0.0))
    z2 = done(V.memset(BP[:, 68:72], 0.0))
    zd = done(V.memset(DD[:, 0:2, :], 0.0))
    part(V.memset(G[:, p, 0:2], 0.5))
    part(V.memset(G[:, p, 10:12], 0.5))
    zp = done(V.memset(PR[:, 3, :], 0.0))
    wait(V, z1, z2, zd)
    wait(A, z1, z2, zd)
    V.wait_ge(T.sem.ld, 16)
    A.wait_ge(T.sem.ld, 16)

    dk = None
    for k in (1, 2, 3):
        lo, hi = 4 - k, 68 + k
        if k == 1:
            left, right, mid = BP[:, lo - 1:hi - 1], BP[:, lo + 1:hi + 1], BP[:, lo:hi]
        else:
            left, right, mid = DD[:, k - 2, lo - 1:hi - 1], DD[:, k - 2, lo + 1:hi + 1], DD[:, k - 2, lo:hi]
            wait(V, dk)
            wait(A, dk)
        sk = done(V.tensor_tensor(SS[:, k - 1, lo:hi], left, right, add))
        tk = done(A.activation(PT[k - 1][:, lo:hi], mid, Ident, scale=2.0))
        if k == 1:
            part(A.activation(J0[:, 0, 4:68], BP[:, 4:68], Square, accum_out=G[:, p, PW:PW + 1]))
        elif k == 2:
            part(A.activation(J0[:, 1, 3:69], DD[:, 0, 3:69], Square, accum_out=G[:, p, PW + 1:PW + 2]))
        else:
            part(A.activation(J0[:, 2, 2:70], DD[:, 1, 2:70], Square, accum_out=G[:, p, PW + 10:PW + 11]))
            part(A.activation(G[:, p, 2:10], DD[:, 0:2, 2:6], Ident))
            part(A.activation(G[:, p, PW + 2:PW + 10], DD[:, 0:2, 66:70], Ident))
        wait(V, tk, sk)
        dk = done(V.tensor_tensor(DD[:, k - 1, lo:hi], SS[:, k - 1, lo:hi], PT[k - 1][:, lo:hi], add))
    part(V.tensor_tensor(G[:, p, PW + 12:PW + 18], SS[:, 2, 65:71], T.PT2[:, 65:71], add))
    part(V.tensor_tensor(G[:, p, 12:18], SS[:, 2, 1:7], T.PT2[:, 1:7], add))
    wait(A, dk)
    part(A.activation(J0[:, 3, 1:71], DD[:, 2, 1:71], Square, accum_out=G[:, p, PW + 11:PW + 12]))
    whole = npk[0]

    def tr(dst_rank, engines, sem, slot):
        d = T.cores[dst_rank]
        rid, pid = topo.addr(d, core)
        return RemoteDMATransfer(dst_ids=[DstId(rid=rid, pnc=pid)], dma_engine_mask=_mask(engines), remote_sem=sem,
                                 src=G[:, p, :], dst=G[:, slot, :])

    off = _bits(topo.mask(core, T.cores[nxt[0]]) & topo.mask(core, T.cores[prv[0]]))
    onl = [e for e in _bits(topo.mask(core, T.cores[partner])) if e not in off]
    half = len(off) // 2
    ea, eb = off[:half], off[half:]
    ep = onl[:half]
    at_next = rank - base
    at_prev = 2 * per + (rank - base)
    g.wait_ge(T.sem.pkg, whole)
    g.remote_dma_fused([tr(nxt[0], ea, T.sem.arrL, at_next), tr(prv[-1], eb, T.sem.arrR, at_prev)], local_sem=T.sem.sent)
    g.remote_dma_fused([tr(nxt[-1], ea, T.sem.arrL, at_next), tr(prv[0], eb, T.sem.arrR, at_prev),
                        tr(partner, ep, T.sem.arrP, p)], local_sem=T.sem.sent)
    if first:
        g.wait_ge(T.sem.arrL, per * half)
        src, d = G[:, 0:per, :], T.cores[nxt[0]]
    else:
        g.wait_ge(T.sem.arrR, per * half)
        src, d = G[:, 2 * per:3 * per, :], T.cores[prv[-1]]
    rid, pid = topo.addr(d, core)
    g.remote_dma(G[:, 3 * per:4 * per, :], src, T.sem.arrD, T.sem.sent, pid, rid, _mask(off))
    g.wait_ge(T.sem.sent, 2 * half + 3 * half + len(off))

    d4 = done(A.activation(T.D4W[:, :], DD[:, 1, 4:68], Ident, scale=-W1))
    A.wait_ge(T.sem.arrL, per * half)
    c8 = done(A.activation(G[:, 8, 0:PW], G[:, 0, 0:PW], Ident))
    V.wait_ge(T.sem.pkg, whole)
    V.wait_ge(T.sem.arrL, per * half)
    V.wait_ge(T.sem.arrR, per * half)
    V.wait_ge(T.sem.arrP, half)
    pe = done(V.tensor_tensor(PE[:, :, :], G[:, 0:5, PW:SW], G[:, 1:6, 0:PW], mul))
    tl = done(V.tensor_scalar(TM[:, 0:2], G[:, p - 1, PW + 8:PW + 10], -W1, None, mul))
    t_r = done(V.tensor_scalar(TM[:, 2:4], G[:, p + 1, 6:8], -W1, None, mul))
    wait(V, d4, tl, t_r)
    hl = done(V.tensor_tensor(T.D4W[:, 0:2], T.D4W[:, 0:2], TM[:, 0:2], add))
    hr = done(V.tensor_tensor(T.D4W[:, 62:64], T.D4W[:, 62:64], TM[:, 2:4], add))
    A.wait_ge(T.sem.pkg, whole)
    A.wait_ge(T.sem.arrR, per * half)
    A.wait_ge(T.sem.arrP, half)
    wait(A, zp, pe)
    e0 = done(A.activation(JE[:, :, 0], G[:, 0:5, PW], Ident, accum_out=G[:, 8, PW:PW + 1]))
    e1 = done(A.activation(JE[:, :, 1:6], PE[:, :, 1:6], Ident, accum_out=PR[:, 3, 1:2]))
    e2 = done(A.activation(JE[:, :, 6:11], PE[:, :, 6:11], Ident, accum_out=PR[:, 3, 6:7]))
    e3 = done(A.activation(JE[:, :, 11:18], PE[:, :, 11:18], Ident, accum_out=PR[:, 3, 11:12]))

    wait(V, c8)
    V.wait_ge(T.sem.arrD, len(off))
    pl = done(V.tensor_tensor(PR[:, 0:3, :], G[:, 5:8, PW:SW], G[:, 6:9, 0:PW], mul))
    wait(A, e0, e1, e2, e3, hl, hr)
    A.wait_ge(T.sem.arrD, len(off))
    r0 = done(A.activation(JR[:, :, 0], G[:, 5:9, PW], Ident, scale=0.5, accum_out=NN[:, 0:1]))
    wait(A, pl)
    r1 = done(A.activation(JR[:, :, 1:6], PR[:, :, 1:6], Ident, scale=W1, accum_out=NN[:, 1:2]))
    r2 = done(A.activation(JR[:, :, 6:11], PR[:, :, 6:11], Ident, scale=W2, accum_out=NN[:, 2:3]))
    r3 = done(A.activation(JR[:, :, 11:18], PR[:, :, 11:18], Ident, scale=W3, accum_out=NN[:, 3:4]))
    wait(V, r0, r1, r2, r3)
    wait(A, r1, r2)
    u1 = done(V.tensor_scalar(UV[:, 0, 0:2], NN[:, 2:4], NN[:, 0:1], None, mul))
    u2 = done(V.tensor_scalar(UV[:, 0, 2:3], NN[:, 3:4], NN[:, 1:2], None, mul))
    v1 = done(A.activation(UV[:, 1, 0:2], NN[:, 1:3], Ident, scale=NN[:, 1:2]))
    v2 = done(A.activation(UV[:, 1, 2:3], NN[:, 2:3], Ident, scale=NN[:, 2:3]))
    wait(V, u1, u2, v1, v2)
    hh = done(V.tensor_tensor_scan(HH[:, 0:3], UV[:, 0, 0:3], UV[:, 1, 0:3], 0.0, add, sub))
    wait(V, hh)
    wait(A, hh)
    rc = done(V.reciprocal(HH[:, 3:4], HH[:, 2:3]))
    t1 = done(A.activation(T.PT3[:, 0:64], BP[:, 4:68], Ident, scale=HH[:, 1:2]))
    t2 = done(A.activation(T.T2[:, :], T.D4W[:, :], Ident, scale=HH[:, 0:1]))
    wait(V, t1, t2)
    sm = done(V.tensor_tensor(T.SB[:, :], T.T2[:, :], T.PT3[:, 0:64], add))
    wait(V, rc, sm)
    yy = done(V.tensor_scalar(T.YB[:, :], T.SB[:, :], HH[:, 3:4], 1.0 / 4.5, mul, mul))
    wait(S, yy)
    S.dma_start(T.y[:, :], T.YB[:, :]).then_inc(T.sem.st, 16)
    S.wait_ge(T.sem.st, 16)
